import numpy as np
import ml_dtypes


def mxq(x, axis, fmt="e4m3"):
    dtype, down = {"e4m3": (ml_dtypes.float8_e4m3fn, 7), "e5m2": (ml_dtypes.float8_e5m2, 14)}[fmt]
    v = np.moveaxis(np.asarray(x, np.float32).astype(ml_dtypes.bfloat16).astype(np.float64), axis, -1)
    blocks = v.reshape(v.shape[:-1] + (-1, 32))
    amax = np.abs(blocks).max(-1, keepdims=True)
    byte = np.maximum(np.where(amax > 0, np.frexp(amax)[1] - 1 + 127, 0) - down, 1)
    scale = np.exp2(byte - 127.0)
    codes = (blocks / scale).astype(np.float32).astype(dtype).astype(np.float64)
    return np.moveaxis((codes * scale).reshape(v.shape), -1, axis)


WIDE = False


def mx_kscale(k):
    if not WIDE:
        return np.ones(k)
    levels = np.array([30, -30])
    if k % 512:
        return np.exp2(np.random.permutation(np.resize(levels, k // 32))).repeat(32)
    a = np.empty((k // 512, 16))
    for p in range(k // 512):
        a[p, :8] = np.random.permutation(np.resize(levels, 8))
        for g in range(8):
            far = levels[np.abs(levels - a[p, g]) >= 10]
            a[p, g + 8] = far[np.random.randint(len(far))]
    return np.exp2(a.ravel()).repeat(32)


BF16 = ml_dtypes.bfloat16


def bf(x):
    return np.asarray(x, np.float32).astype(BF16)


def f64(x):
    return np.asarray(x).astype(np.float64)


E2M1 = np.array([0.0, 0.5, 1.0, 1.5, 2.0, 3.0, 4.0, 6.0, -0.0, -0.5, -1.0, -1.5, -2.0, -3.0, -4.0, -6.0])


def pack_weight(w, fmt):
    k, n = w.shape
    w = f64(bf(w)).reshape(k // 32, 32, n)
    amax = np.abs(w).max(1)
    if fmt == "e4m3":
        byte = np.frexp(amax)[1] - 1 + 127 - 7
    else:
        mant, ex = np.frexp(amax / 6.0)
        byte = np.where(mant > 0.5, ex, ex - 1) + 127
    byte = np.clip(np.where(amax > 0, byte, 1), 1, 254)
    scaled = (w * np.exp2(127.0 - byte)[:, None, :]).reshape(k, n).astype(np.float32)
    by_word = np.ascontiguousarray(scaled.reshape(k // 512, 128, 4, n).transpose(0, 1, 3, 2))
    if fmt == "e4m3":
        words = by_word.astype(ml_dtypes.float8_e4m3fn).view(np.uint8)
    else:
        c = by_word.astype(ml_dtypes.float4_e2m1fn).view(np.uint8) & 0xF
        words = c[..., 0::2] | (c[..., 1::2] << 4)
    return np.ascontiguousarray(words), np.ascontiguousarray(byte.astype(np.uint8).reshape(k // 512, 16, n))


def unpack_weight(words, scales, fmt):
    g, p, n, _ = words.shape
    if fmt == "e4m3":
        vals = np.ascontiguousarray(words).view(ml_dtypes.float8_e4m3fn).astype(np.float64)
    else:
        nib = np.empty((g, p, n, 4), np.uint8)
        nib[..., 0::2] = words & 0xF
        nib[..., 1::2] = words >> 4
        vals = E2M1[nib]
    vals = vals * np.repeat(np.exp2(scales.astype(np.float64) - 127.0), 8, axis=1)[..., None]
    return vals.transpose(0, 1, 3, 2).reshape(g * 512, n)
def pack4(w):
    words, scales = pack_weight(w, "e2m1")
    return words.reshape(words.shape[0], 128, -1), scales


def unpack4(words, scales):
    return unpack_weight(words.reshape(words.shape[0], 128, -1, 2), scales, "e2m1")


M, K, N, R = 1024, 2048, 1536, 512


def setup_inputs():
    s, t = mx_kscale(K), mx_kscale(N)
    common = 0.5 * np.random.standard_normal((1, K))
    x = (np.random.standard_normal((M, K)) + common) * s
    w = np.random.standard_normal((K, N)) / np.sqrt(K) / s[:, None]
    w_words, w_scales = pack4(w)
    rel = (1 + 0.1 * np.random.standard_normal(N)) * t
    model = np.abs(np.random.standard_normal((N, R))) / np.sqrt(N) / t[:, None]
    return {"x": bf(x),
            "w_words": w_words,
            "w_scales": w_scales,
            "rel": bf(rel),
            "model": bf(model)}


def reference(x, w_words, w_scales, rel, model):
    sim = mxq(f64(x), 1, "e4m3") @ unpack4(w_words, w_scales)
    d = sim.mean(axis=1, keepdims=True) - sim
    d = d * f64(rel)
    o = mxq(d, 1, "e5m2") @ mxq(f64(model), 0, "e4m3")
    return o - o.mean(axis=0, keepdims=True)

@@ -1,0 +1,348 @@
+from contextlib import ExitStack
+
+import concourse.mybir as mybir
+from concourse.masks import make_identity
+
+M, K, N, R = 1024, 2048, 1536, 512
+FLOPS = 2 * M * K * N + 2 * M * N * R
+
+F32 = mybir.dt.float32
+BF16 = mybir.dt.bfloat16
+I32 = mybir.dt.int32
+U32 = mybir.dt.uint32
+U8 = mybir.dt.uint8
+E4M3 = mybir.dt.float8_e4m3fn_x4
+E5M2 = mybir.dt.float8_e5m2_x4
+E2M1 = mybir.dt.float4_e2m1fn_x4
+ALU = mybir.AluOpType
+IDENTITY = mybir.ActivationFunctionType.Identity
+
+P = 128
+BANK = 512
+TILES = M // P
+KG = K // 512
+NG = N // 512
+
+
+def tile_centred_pattern_distances_s9_kernel(tc, x, w_words, w_scales, rel, model, out):
+    nc = tc.nc
+    with ExitStack() as ctx:
+        keep = ctx.enter_context(tc.tile_pool(name="keep", bufs=1))
+        work = ctx.enter_context(tc.tile_pool(name="work", bufs=3))
+        psum = ctx.enter_context(tc.psum_pool(name="psum", bufs=1))
+        ctx.enter_context(tc.manual_schedule())
+
+        sum_banks, turn_banks = [], []
+
+        def sum_bank():
+            bank = psum.tile([P, BANK], F32, name="sum_bank", tag="sum%d" % (len(sum_banks) % 4))
+            sum_banks.append(bank)
+            return bank
+
+        def turn_bank():
+            bank = psum.tile([P, BANK], F32, name="turn_bank", tag="turn%d" % (len(turn_banks) % 4))
+            turn_banks.append(bank)
+            return bank
+
+        ones = keep.tile([P, P], F32, name="ones")
+        nc.vector.memset(ones[:], 1.0)
+        w_plane = keep.tile([P, KG, N], U8, name="w_plane", align_bytes=64)
+        nc.vector.memset(w_plane[:].bitcast(I32), 0)
+        ident_bf = keep.tile([P, P], BF16, name="ident_bf")
+        make_identity(nc, ident_bf[:])
+        ident = keep.tile([P, P], F32, name="ident")
+        make_identity(nc, ident[:])
+        mean_weights = keep.tile([P, P], F32, name="mean_weights")
+        nc.scalar.activation(out=mean_weights[:], in_=ones[:], func=IDENTITY, scale=1.0 / M)
+
+        rel_cols = keep.tile([P, NG * 4], BF16, name="rel_cols")
+        nc.sync.dma_start(
+            out=rel_cols[:].rearrange("p (g t) -> p g t", t=4),
+            in_=rel.rearrange("(g p t) -> p g t", p=P, t=4),
+        )
+        x_rows, w_codes, model_rows = {}, {}, {}
+
+        def load_x(i):
+            x_rows[i] = keep.tile([P, K], BF16, name="x_rows", tag="x%d" % i)
+            nc.sync.dma_start(out=x_rows[i][:], in_=x[i * P : (i + 1) * P, :])
+
+        def load_model(g):
+            model_rows[g] = keep.tile([P, 4, R], BF16, name="model_rows", tag="model%d" % g)
+            nc.sync.dma_start(
+                out=model_rows[g][:], in_=model[512 * g : 512 * (g + 1), :].rearrange("(p t) r -> p t r", t=4)
+            )
+
+        load_x(0)
+        load_x(1)
+        for q in range(4):
+            nc.sync.dma_start(
+                out=w_plane[32 * q : 32 * q + 4, :, :].bitcast(I32),
+                in_=w_scales[:, 4 * q : 4 * q + 4, :].bitcast(I32).rearrange("g r n -> r g n"),
+            )
+        for g in range(KG):
+            w_codes[g] = keep.tile([P, 2 * N], U8, name="w_codes", tag="w%d" % g, align_bytes=64)
+            nc.sync.dma_start(out=w_codes[g][:].bitcast(I32), in_=w_words[g].bitcast(I32))
+        for g in range(NG):
+            load_model(g)
+            load_x(2 + g)
+        for i in range(2 + NG, TILES):
+            load_x(i)
+
+        neg_rel = {}
+        for g in range(NG):
+            bank = sum_bank()
+            for t in range(4):
+                m = 4 * g + t
+                nc.tensor.matmul(
+                    bank[:, t * P : (t + 1) * P],
+                    lhsT=rel_cols[:, m : m + 1].to_broadcast([P, P]),
+                    rhs=ident_bf[:],
+                    start=True,
+                    stop=True,
+                )
+            neg_rel[g] = keep.tile([P, BANK], BF16, name="neg_rel", tag="neg_rel%d" % g)
+            nc.vector.tensor_scalar(
+                out=neg_rel[g][:].rearrange("p (u c e) -> p u c e", u=2, e=2),
+                in0=bank[:].rearrange("p (u e c) -> p u c e", u=2, e=2),
+                scalar1=-1.0,
+                scalar2=None,
+                op0=ALU.mult,
+            )
+
+        x_banks, x_grouped, x_codes, x_plane = {}, {}, {}, {}
+
+        def x_turn(i):
+            words = x_rows[i][:].bitcast(F32)
+            for h in range(2):
+                x_banks[i, h] = turn_bank()
+                for j in range(4):
+                    g, u = 2 * h + j // 2, j % 2
+                    nc.tensor.transpose(
+                        x_banks[i, h][:, j * P : (j + 1) * P], words[:, 256 * g + u : 256 * (g + 1) : 2], ident[:]
+                    )
+
+        def x_copy(i, h):
+            if h == 0:
+                x_grouped[i] = work.tile([P, K], BF16, name="x_grouped", align_bytes=64)
+            words = x_grouped[i][:].bitcast(F32)
+            nc.scalar.copy(
+                out=words[:, h * BANK : (h + 1) * BANK].rearrange("p (g r u) -> p g r u", g=2, u=2),
+                in_=x_banks[i, h][:].rearrange("p (g u r) -> p g r u", g=2, u=2),
+            )
+
+        def x_quant(i):
+            x_codes[i] = work.tile([P, KG * P], U32, name="x_codes", align_bytes=64)
+            x_plane[i] = work.tile([P, KG * P], U8, name="x_plane", align_bytes=64)
+            nc.vector.quantize_mx(out=x_codes[i][:].bitcast(E4M3), scales=x_plane[i][:], in_=x_grouped[i][:])
+
+        model_grouped, model_codes, model_plane = {}, {}, {}
+
+        def model_group(g):
+            model_grouped[g] = keep.tile([P, 4 * R], BF16, name="model_grouped", tag="mg%d" % g, align_bytes=64)
+            nc.vector.tensor_copy(
+                out=model_grouped[g][:].rearrange("p (c i t) -> p c t i", i=4, t=4),
+                in_=model_rows[g][:].rearrange("p t (c i) -> p c t i", i=4),
+            )
+
+        def model_quant(g):
+            model_codes[g] = keep.tile([P, R], U32, name="model_codes", tag="mc%d" % g, align_bytes=64)
+            model_plane[g] = keep.tile([P, R], U8, name="model_plane", tag="mp%d" % g, align_bytes=64)
+            nc.vector.quantize_mx(
+                out=model_codes[g][:].bitcast(E4M3), scales=model_plane[g][:], in_=model_grouped[g][:]
+            )
+
+        sim, row_mean, d_rows = {}, {}, {}
+
+        def sim_pass(i, nb, g):
+            if g == 0:
+                sim[i, nb] = sum_bank()
+            nc.tensor.matmul_mx(
+                out=sim[i, nb][:],
+                lhsT=x_codes[i][:, g * P : (g + 1) * P].bitcast(E4M3),
+                lhsT_scale=x_plane[i][:, g * P : (g + 1) * P],
+                rhs=w_codes[g][:, 2 * BANK * nb : 2 * BANK * (nb + 1)].bitcast(E2M1),
+                rhs_scale=w_plane[:, g, BANK * nb : BANK * (nb + 1)],
+                start=(g == 0),
+                stop=(g == KG - 1),
+            )
+
+        def sim_bank(i, nb):
+            for g in range(KG):
+                sim_pass(i, nb, g)
+
+        def row_sum(i, nb):
+            unused = work.tile([P, BANK], BF16, name="unused")
+            total = work.tile([P, 1], F32, name="total", bufs=6)
+            nc.scalar.activation(
+                out=unused[:],
+                in_=sim[i, nb][:],
+                func=IDENTITY,
+                scale=1.0 / (N * BANK ** (NG - 1 - nb)),
+                bias=row_mean[i][:] if nb else 0.0,
+                accum_out=total[:],
+            )
+            row_mean[i] = total
+
+        def d_make(i, g):
+            d_rows[i, g] = work.tile([P, BANK], BF16, name="d_rows", bufs=9)
+            for u in range(2):
+                half = slice(256 * u, 256 * (u + 1))
+                nc.vector.scalar_tensor_tensor(
+                    out=d_rows[i, g][:, half].rearrange("p (c e) -> p c e", e=2),
+                    in0=sim[i, g][:].rearrange("p (c u e) -> p u c e", u=2, e=2)[:, u],
+                    scalar=row_mean[i][:],
+                    in1=neg_rel[g][:, half].rearrange("p (c e) -> p c e", e=2),
+                    op0=ALU.subtract,
+                    op1=ALU.mult,
+                )
+
+        d_banks, d_grouped, d_codes, d_plane = {}, {}, {}, {}
+
+        def d_turn(i, groups):
+            d_banks[i, groups] = turn_bank()
+            for j, g in enumerate(groups):
+                words = d_rows[i, g][:].bitcast(F32)
+                for u in range(2):
+                    col = (2 * j + u) * P
+                    nc.tensor.transpose(d_banks[i, groups][:, col : col + P], words[:, u * P : (u + 1) * P], ident[:])
+
+        def d_copy(i, groups):
+            n = len(groups)
+            d_grouped[i, groups] = work.tile([P, n * 512], BF16, name="d_grouped", bufs=4, align_bytes=64)
+            nc.scalar.copy(
+                out=d_grouped[i, groups][:].bitcast(F32).rearrange("p (g r u) -> p g r u", g=n, u=2),
+                in_=d_banks[i, groups][:, : n * 2 * P].rearrange("p (g u r) -> p g r u", g=n, u=2),
+            )
+
+        def d_quant(i, groups):
+            n = len(groups)
+            codes = work.tile([P, n * P], U32, name="d_codes", bufs=8, align_bytes=64)
+            plane = work.tile([P, n * P], U8, name="d_plane", bufs=8, align_bytes=64)
+            nc.vector.quantize_mx(out=codes[:].bitcast(E5M2), scales=plane[:], in_=d_grouped[i, groups][:])
+            for j, g in enumerate(groups):
+                d_codes[i, g] = codes[:, j * P : (j + 1) * P]
+                d_plane[i, g] = plane[:, j * P : (j + 1) * P]
+
+        o_banks, o_rows = {}, {}
+        o_total = keep.tile([P, R], F32, name="o_total")
+
+        def scores(i):
+            o_banks[i] = sum_bank()
+            for g in range(NG):
+                nc.tensor.matmul_mx(
+                    out=o_banks[i][:],
+                    lhsT=d_codes[i, g].bitcast(E5M2),
+                    lhsT_scale=d_plane[i, g],
+                    rhs=model_codes[g][:].bitcast(E4M3),
+                    rhs_scale=model_plane[g][:],
+                    start=(g == 0),
+                    stop=(g == NG - 1),
+                )
+
+        def o_copy(i):
+            o_rows[i] = keep.tile([P, R], F32, name="o_rows", tag="o%d" % i)
+            nc.scalar.copy(out=o_rows[i][:], in_=o_banks[i][:])
+
+        def o_add(i, source):
+            if i > 0:
+                so_far = o_rows[0] if i == 1 else o_total
+                nc.vector.tensor_tensor(out=o_total[:], in0=so_far[:], in1=source[:], op=ALU.add)
+
+        PAIR, SINGLE = (0, 1), (2,)
+        LAST = TILES - 1
+
+        for i in range(2):
+            x_turn(i)
+            x_copy(i, 0)
+            x_copy(i, 1)
+            x_quant(i)
+        for g in range(KG):
+            for nb in range(NG):
+                sim_pass(0, nb, g)
+        model_group(0)
+        for nb in range(NG):
+            row_sum(0, nb)
+        sim_bank(1, 0)
+        x_turn(2)
+        for g in range(NG):
+            d_make(0, g)
+        model_quant(0)
+
+        for i in range(1, TILES):
+            if i == 4:
+                scores(1)
+            if i >= 2:
+                d_copy(i - 2, PAIR)
+                d_copy(i - 2, SINGLE)
+                d_quant(i - 2, PAIR)
+                d_quant(i - 2, SINGLE)
+            if i == 4:
+                o_copy(1)
+                o_add(1, o_rows[1])
+            if i > 1:
+                sim_bank(i, 0)
+            row_sum(i, 0)
+            if i < LAST:
+                x_copy(i + 1, 0)
+            sim_bank(i, 1)
+            row_sum(i, 1)
+            if i < LAST:
+                x_copy(i + 1, 1)
+            if i == 2:
+                model_group(2)
+            if i < LAST:
+                x_quant(i + 1)
+            if i == 1:
+                model_group(1)
+            sim_bank(i, 2)
+            row_sum(i, 2)
+            if i == LAST:
+                break
+            for g in range(NG):
+                d_make(i, g)
+            if i in (1, 2):
+                model_quant(i)
+            if i >= 3:
+                j = 0 if i == 3 else i - 2
+                scores(j)
+                o_copy(j)
+                o_add(j, o_rows[j])
+            d_turn(i - 1, PAIR)
+            d_turn(i - 1, SINGLE)
+            if i + 2 < TILES:
+                x_turn(i + 2)
+
+        d_turn(LAST - 1, PAIR)
+        d_turn(LAST - 1, SINGLE)
+        d_copy(LAST - 1, PAIR)
+        d_copy(LAST - 1, SINGLE)
+        scores(LAST - 2)
+        d_make(LAST, 0)
+        d_quant(LAST - 1, PAIR)
+        d_quant(LAST - 1, SINGLE)
+        d_turn(LAST, (0,))
+        d_copy(LAST, (0,))
+        o_copy(LAST - 2)
+        d_make(LAST, 1)
+        scores(LAST - 1)
+        o_copy(LAST - 1)
+        d_turn(LAST, (1,))
+        d_copy(LAST, (1,))
+        d_make(LAST, 2)
+        d_turn(LAST, (2,))
+        d_copy(LAST, (2,))
+        d_quant(LAST, (0,))
+        o_add(LAST - 2, o_rows[LAST - 2])
+        d_quant(LAST, (1,))
+        d_quant(LAST, (2,))
+        o_add(LAST - 1, o_rows[LAST - 1])
+        scores(LAST)
+        o_add(LAST, o_banks[LAST])
+        o_copy(LAST)
+
+        col_mean = turn_bank()
+        nc.tensor.matmul(col_mean[:], lhsT=mean_weights[:], rhs=o_total[:], start=True, stop=True)
+        for i in range(TILES):
+            result = work.tile([P, R], F32, name="result", bufs=TILES)
+            nc.vector.tensor_tensor(out=result[:], in0=o_rows[i][:], in1=col_mean[:], op=ALU.subtract)
+            nc.sync.dma_start(out=out[i * P : (i + 1) * P, :], in_=result[:])

@@ -18,10 +18,15 @@ ALU = mybir.AluOpType
 IDENTITY = mybir.ActivationFunctionType.Identity
 
 P = 128
-BANK = 512
+GROUP = 512
 TILES = M // P
-KG = K // 512
-NG = N // 512
+LAST = TILES - 1
+X_GROUPS = K // GROUP
+D_GROUPS = N // GROUP
+FRONT, BACK = (0, 1), (2,)
+SCORE_LAG = 4
+SORT_LEAD = 3
+WARM_UP = (3, 1, 2)
 
 
 def tile_centred_pattern_distances_s9_kernel(tc, x, w_words, w_scales, rel, model, out):
@@ -32,161 +37,187 @@ def tile_centred_pattern_distances_s9_kernel(tc, x, w_words, w_scales, rel, mode
         psum = ctx.enter_context(tc.psum_pool(name="psum", bufs=1))
         ctx.enter_context(tc.manual_schedule())
 
-        sum_banks, turn_banks = [], []
+        free_banks, bank_of = list(range(8)), {}
 
-        def sum_bank():
-            bank = psum.tile([P, BANK], F32, name="sum_bank", tag="sum%d" % (len(sum_banks) % 4))
-            sum_banks.append(bank)
+        def take_bank(owner):
+            bank_of[owner] = free_banks.pop(0)
+            bank = psum.tile([P, GROUP], F32, name="bank", tag="bank%d" % bank_of[owner])
             return bank
 
-        def turn_bank():
-            bank = psum.tile([P, BANK], F32, name="turn_bank", tag="turn%d" % (len(turn_banks) % 4))
-            turn_banks.append(bank)
-            return bank
+        def give_bank(owner):
+            free_banks.append(bank_of.pop(owner))
 
+        zeros = keep.tile([P, GROUP], BF16, name="zeros")
+        nc.vector.memset(zeros[:], 0.0)
         ones = keep.tile([P, P], F32, name="ones")
         nc.vector.memset(ones[:], 1.0)
-        w_plane = keep.tile([P, KG, N], U8, name="w_plane", align_bytes=64)
-        nc.vector.memset(w_plane[:].bitcast(I32), 0)
-        ident_bf = keep.tile([P, P], BF16, name="ident_bf")
-        make_identity(nc, ident_bf[:])
+        w_planes = []
+        for banks in (1, D_GROUPS - 1):
+            plane = keep.tile([P, X_GROUPS, banks * GROUP], U8, name="w_plane", tag="w_plane%d" % banks, align_bytes=64)
+            nc.vector.memset(plane[:].bitcast(I32), 0)
+            w_planes.append(plane)
         ident = keep.tile([P, P], F32, name="ident")
         make_identity(nc, ident[:])
-        mean_weights = keep.tile([P, P], F32, name="mean_weights")
-        nc.scalar.activation(out=mean_weights[:], in_=ones[:], func=IDENTITY, scale=1.0 / M)
-
-        rel_cols = keep.tile([P, NG * 4], BF16, name="rel_cols")
-        nc.sync.dma_start(
+        ident_bf = keep.tile([P, P], BF16, name="ident_bf")
+        make_identity(nc, ident_bf[:])
+        rel_cols = keep.tile([P, D_GROUPS * 4], BF16, name="rel_cols")
+        nc.scalar.dma_start(
             out=rel_cols[:].rearrange("p (g t) -> p g t", t=4),
             in_=rel.rearrange("(g p t) -> p g t", p=P, t=4),
         )
+        mean_weights = keep.tile([P, P], F32, name="mean_weights")
+        nc.scalar.activation(out=mean_weights[:], in_=ones[:], func=IDENTITY, scale=1.0 / M)
+
         x_rows, w_codes, model_rows = {}, {}, {}
 
         def load_x(i):
-            x_rows[i] = keep.tile([P, K], BF16, name="x_rows", tag="x%d" % i)
+            x_rows[i] = keep.tile([P, K], BF16, name="x_rows", tag="x_rows%d" % i)
             nc.sync.dma_start(out=x_rows[i][:], in_=x[i * P : (i + 1) * P, :])
 
-        def load_model(g):
-            model_rows[g] = keep.tile([P, 4, R], BF16, name="model_rows", tag="model%d" % g)
+        def load_w_scales(plane, first):
+            cols = slice(first, first + plane.shape[2])
+            for q in range(4):
+                nc.sync.dma_start(
+                    out=plane[32 * q : 32 * q + 4, :, :].bitcast(I32),
+                    in_=w_scales[:, 4 * q : 4 * q + 4, cols].bitcast(I32).rearrange("g r n -> r g n"),
+                )
+
+        def load_w_codes(b):
+            w_codes[b] = keep.tile([P, X_GROUPS, 2 * GROUP], U8, name="w_codes", tag="w_codes%d" % b, align_bytes=64)
             nc.sync.dma_start(
-                out=model_rows[g][:], in_=model[512 * g : 512 * (g + 1), :].rearrange("(p t) r -> p t r", t=4)
+                out=w_codes[b][:].bitcast(I32),
+                in_=w_words[:, :, 2 * GROUP * b : 2 * GROUP * (b + 1)].bitcast(I32).rearrange("g p n -> p g n"),
+            )
+
+        def load_model(g):
+            model_rows[g] = keep.tile([P, 4, R], BF16, name="model_rows", tag="model_rows%d" % g)
+            nc.sync.dma_start(
+                out=model_rows[g][:], in_=model[GROUP * g : GROUP * (g + 1), :].rearrange("(p t) r -> p t r", t=4)
             )
 
         load_x(0)
         load_x(1)
-        for q in range(4):
-            nc.sync.dma_start(
-                out=w_plane[32 * q : 32 * q + 4, :, :].bitcast(I32),
-                in_=w_scales[:, 4 * q : 4 * q + 4, :].bitcast(I32).rearrange("g r n -> r g n"),
-            )
-        for g in range(KG):
-            w_codes[g] = keep.tile([P, 2 * N], U8, name="w_codes", tag="w%d" % g, align_bytes=64)
-            nc.sync.dma_start(out=w_codes[g][:].bitcast(I32), in_=w_words[g].bitcast(I32))
-        for g in range(NG):
+        load_w_scales(w_planes[0], 0)
+        load_w_codes(0)
+        load_w_scales(w_planes[1], GROUP)
+        load_w_codes(1)
+        load_x(2)
+        load_w_codes(2)
+        for g in range(D_GROUPS):
             load_model(g)
-            load_x(2 + g)
-        for i in range(2 + NG, TILES):
+            load_x(3 + g)
+        for i in range(3 + D_GROUPS, TILES):
             load_x(i)
 
-        neg_rel = {}
-        for g in range(NG):
-            bank = sum_bank()
-            for t in range(4):
-                m = 4 * g + t
-                nc.tensor.matmul(
-                    bank[:, t * P : (t + 1) * P],
-                    lhsT=rel_cols[:, m : m + 1].to_broadcast([P, P]),
-                    rhs=ident_bf[:],
-                    start=True,
-                    stop=True,
-                )
-            neg_rel[g] = keep.tile([P, BANK], BF16, name="neg_rel", tag="neg_rel%d" % g)
-            nc.vector.tensor_scalar(
-                out=neg_rel[g][:].rearrange("p (u c e) -> p u c e", u=2, e=2),
-                in0=bank[:].rearrange("p (u e c) -> p u c e", u=2, e=2),
-                scalar1=-1.0,
-                scalar2=None,
-                op0=ALU.mult,
-            )
+        def w_scale(g, b):
+            return w_planes[0][:, g, :] if b == 0 else w_planes[1][:, g, GROUP * (b - 1) : GROUP * b]
 
-        x_banks, x_grouped, x_codes, x_plane = {}, {}, {}, {}
+        def keep_warm(bank, count):
+            for j in range(count):
+                nc.tensor.matmul(bank[:], lhsT=zeros[:, :P], rhs=zeros[:], start=True, stop=True)
+
+        neg_rel = {}
+
+        def spread_rel(g):
+            bank = take_bank("rel")
+            for t in range(4):
+                column = rel_cols[:, 4 * g + t : 4 * g + t + 1].to_broadcast([P, P])
+                nc.tensor.matmul(bank[:, t * P : (t + 1) * P], lhsT=column, rhs=ident_bf[:], start=True, stop=True)
+            neg_rel[g] = keep.tile([P, GROUP], BF16, name="neg_rel", tag="neg_rel%d" % g)
+            nc.scalar.activation(
+                out=neg_rel[g][:].rearrange("p (u c e) -> p u c e", u=2, e=2),
+                in_=bank[:].rearrange("p (u e c) -> p u c e", u=2, e=2),
+                func=IDENTITY,
+                scale=-1.0,
+            )
+            give_bank("rel")
+
+        x_sorted, x_banks, x_turned, x_codes, x_scales = {}, {}, {}, {}, {}
+
+        def x_sort(i, copy):
+            x_sorted[i] = work.tile([P, K // 2], F32, name="x_sorted")
+            copy(
+                out=x_sorted[i][:].rearrange("p (g u c) -> p g u c", g=X_GROUPS, u=2),
+                in_=x_rows[i][:].bitcast(F32).rearrange("p (g c u) -> p g u c", g=X_GROUPS, u=2),
+            )
 
         def x_turn(i):
-            words = x_rows[i][:].bitcast(F32)
             for h in range(2):
-                x_banks[i, h] = turn_bank()
+                x_banks[i, h] = take_bank(("x", i, h))
                 for j in range(4):
                     g, u = 2 * h + j // 2, j % 2
-                    nc.tensor.transpose(
-                        x_banks[i, h][:, j * P : (j + 1) * P], words[:, 256 * g + u : 256 * (g + 1) : 2], ident[:]
-                    )
+                    if i == 0:
+                        pairs = x_rows[i][:].bitcast(F32)[:, 2 * P * g + u : 2 * P * (g + 1) : 2]
+                    else:
+                        pairs = x_sorted[i][:, (2 * g + u) * P : (2 * g + u + 1) * P]
+                    nc.tensor.transpose(x_banks[i, h][:, j * P : (j + 1) * P], pairs, ident[:])
 
-        def x_copy(i, h):
-            if h == 0:
-                x_grouped[i] = work.tile([P, K], BF16, name="x_grouped", align_bytes=64)
-            words = x_grouped[i][:].bitcast(F32)
-            nc.scalar.copy(
-                out=words[:, h * BANK : (h + 1) * BANK].rearrange("p (g r u) -> p g r u", g=2, u=2),
-                in_=x_banks[i, h][:].rearrange("p (g u r) -> p g r u", g=2, u=2),
-            )
+        def x_finish(i):
+            for h in range(2):
+                x_turned[i, h] = work.tile([P, K // 2], BF16, name="x_turned", bufs=4, align_bytes=64)
+                nc.scalar.copy(
+                    out=x_turned[i, h][:].bitcast(F32).rearrange("p (g r u) -> p g r u", g=2, u=2),
+                    in_=x_banks[i, h][:].rearrange("p (g u r) -> p g r u", g=2, u=2),
+                )
+                give_bank(("x", i, h))
 
-        def x_quant(i):
-            x_codes[i] = work.tile([P, KG * P], U32, name="x_codes", align_bytes=64)
-            x_plane[i] = work.tile([P, KG * P], U8, name="x_plane", align_bytes=64)
-            nc.vector.quantize_mx(out=x_codes[i][:].bitcast(E4M3), scales=x_plane[i][:], in_=x_grouped[i][:])
+        def x_quantise(i):
+            for h in range(2):
+                x_codes[i, h] = work.tile([P, 2 * P], U32, name="x_codes", bufs=6, align_bytes=64)
+                x_scales[i, h] = work.tile([P, 2 * P], U8, name="x_scales", bufs=6, align_bytes=64)
+                nc.vector.quantize_mx(
+                    out=x_codes[i, h][:].bitcast(E4M3), scales=x_scales[i, h][:], in_=x_turned[i, h][:]
+                )
 
-        model_grouped, model_codes, model_plane = {}, {}, {}
+        model_words, model_codes, model_scales = {}, {}, {}
 
-        def model_group(g):
-            model_grouped[g] = keep.tile([P, 4 * R], BF16, name="model_grouped", tag="mg%d" % g, align_bytes=64)
+        def model_interleave(g):
+            model_words[g] = keep.tile([P, 4 * R], BF16, name="model_words", tag="model_words%d" % g, align_bytes=64)
             nc.vector.tensor_copy(
-                out=model_grouped[g][:].rearrange("p (c i t) -> p c t i", i=4, t=4),
+                out=model_words[g][:].rearrange("p (c i t) -> p c t i", i=4, t=4),
                 in_=model_rows[g][:].rearrange("p t (c i) -> p c t i", i=4),
             )
 
-        def model_quant(g):
-            model_codes[g] = keep.tile([P, R], U32, name="model_codes", tag="mc%d" % g, align_bytes=64)
-            model_plane[g] = keep.tile([P, R], U8, name="model_plane", tag="mp%d" % g, align_bytes=64)
+        def model_quantise(g):
+            model_codes[g] = keep.tile([P, R], U32, name="model_codes", tag="model_codes%d" % g, align_bytes=64)
+            model_scales[g] = keep.tile([P, R], U8, name="model_scales", tag="model_scales%d" % g, align_bytes=64)
             nc.vector.quantize_mx(
-                out=model_codes[g][:].bitcast(E4M3), scales=model_plane[g][:], in_=model_grouped[g][:]
+                out=model_codes[g][:].bitcast(E4M3), scales=model_scales[g][:], in_=model_words[g][:]
             )
 
         sim, row_mean, d_rows = {}, {}, {}
 
-        def sim_pass(i, nb, g):
-            if g == 0:
-                sim[i, nb] = sum_bank()
-            nc.tensor.matmul_mx(
-                out=sim[i, nb][:],
-                lhsT=x_codes[i][:, g * P : (g + 1) * P].bitcast(E4M3),
-                lhsT_scale=x_plane[i][:, g * P : (g + 1) * P],
-                rhs=w_codes[g][:, 2 * BANK * nb : 2 * BANK * (nb + 1)].bitcast(E2M1),
-                rhs_scale=w_plane[:, g, BANK * nb : BANK * (nb + 1)],
-                start=(g == 0),
-                stop=(g == KG - 1),
-            )
+        def sim_bank(i, b):
+            sim[i, b] = take_bank(("sim", i, b))
+            for g in range(X_GROUPS):
+                probes = slice(g % 2 * P, (g % 2 + 1) * P)
+                nc.tensor.matmul_mx(
+                    out=sim[i, b][:],
+                    lhsT=x_codes[i, g // 2][:, probes].bitcast(E4M3),
+                    lhsT_scale=x_scales[i, g // 2][:, probes],
+                    rhs=w_codes[b][:, g, :].bitcast(E2M1),
+                    rhs_scale=w_scale(g, b),
+                    start=(g == 0),
+                    stop=(g == X_GROUPS - 1),
+                )
 
-        def sim_bank(i, nb):
-            for g in range(KG):
-                sim_pass(i, nb, g)
-
-        def row_sum(i, nb):
-            unused = work.tile([P, BANK], BF16, name="unused")
-            total = work.tile([P, 1], F32, name="total", bufs=6)
+        def row_sum(i, b):
+            unread = work.tile([P, GROUP], BF16, name="unread")
+            total = work.tile([P, 1], F32, name="total", bufs=8)
             nc.scalar.activation(
-                out=unused[:],
-                in_=sim[i, nb][:],
+                out=unread[:],
+                in_=sim[i, b][:],
                 func=IDENTITY,
-                scale=1.0 / (N * BANK ** (NG - 1 - nb)),
-                bias=row_mean[i][:] if nb else 0.0,
+                scale=1.0 / (N * GROUP ** (D_GROUPS - 1 - b)),
+                bias=row_mean[i][:] if b else 0.0,
                 accum_out=total[:],
             )
             row_mean[i] = total
 
         def d_make(i, g):
-            d_rows[i, g] = work.tile([P, BANK], BF16, name="d_rows", bufs=9)
+            d_rows[i, g] = work.tile([P, GROUP], BF16, name="d_rows", bufs=9)
             for u in range(2):
-                half = slice(256 * u, 256 * (u + 1))
+                half = slice(2 * P * u, 2 * P * (u + 1))
                 nc.vector.scalar_tensor_tensor(
                     out=d_rows[i, g][:, half].rearrange("p (c e) -> p c e", e=2),
                     in0=sim[i, g][:].rearrange("p (c u e) -> p u c e", u=2, e=2)[:, u],
@@ -195,153 +226,178 @@ def tile_centred_pattern_distances_s9_kernel(tc, x, w_words, w_scales, rel, mode
                     op0=ALU.subtract,
                     op1=ALU.mult,
                 )
+            give_bank(("sim", i, g))
 
-        d_banks, d_grouped, d_codes, d_plane = {}, {}, {}, {}
+        d_banks, d_turned, d_codes, d_scales = {}, {}, {}, {}
 
         def d_turn(i, groups):
-            d_banks[i, groups] = turn_bank()
+            d_banks[i, groups] = take_bank(("d", i, groups))
             for j, g in enumerate(groups):
-                words = d_rows[i, g][:].bitcast(F32)
+                pairs = d_rows[i, g][:].bitcast(F32)
                 for u in range(2):
                     col = (2 * j + u) * P
-                    nc.tensor.transpose(d_banks[i, groups][:, col : col + P], words[:, u * P : (u + 1) * P], ident[:])
+                    nc.tensor.transpose(d_banks[i, groups][:, col : col + P], pairs[:, u * P : (u + 1) * P], ident[:])
 
-        def d_copy(i, groups):
+        def d_finish(i, groups):
             n = len(groups)
-            d_grouped[i, groups] = work.tile([P, n * 512], BF16, name="d_grouped", bufs=4, align_bytes=64)
+            d_turned[i, groups] = work.tile([P, n * GROUP], BF16, name="d_turned", bufs=4, align_bytes=64)
             nc.scalar.copy(
-                out=d_grouped[i, groups][:].bitcast(F32).rearrange("p (g r u) -> p g r u", g=n, u=2),
+                out=d_turned[i, groups][:].bitcast(F32).rearrange("p (g r u) -> p g r u", g=n, u=2),
                 in_=d_banks[i, groups][:, : n * 2 * P].rearrange("p (g u r) -> p g r u", g=n, u=2),
             )
+            give_bank(("d", i, groups))
 
-        def d_quant(i, groups):
+        def d_quantise(i, groups):
             n = len(groups)
-            codes = work.tile([P, n * P], U32, name="d_codes", bufs=8, align_bytes=64)
-            plane = work.tile([P, n * P], U8, name="d_plane", bufs=8, align_bytes=64)
-            nc.vector.quantize_mx(out=codes[:].bitcast(E5M2), scales=plane[:], in_=d_grouped[i, groups][:])
+            codes = work.tile([P, n * P], U32, name="d_codes", bufs=10, align_bytes=64)
+            scales = work.tile([P, n * P], U8, name="d_scales", bufs=10, align_bytes=64)
+            nc.vector.quantize_mx(out=codes[:].bitcast(E5M2), scales=scales[:], in_=d_turned[i, groups][:])
             for j, g in enumerate(groups):
                 d_codes[i, g] = codes[:, j * P : (j + 1) * P]
-                d_plane[i, g] = plane[:, j * P : (j + 1) * P]
+                d_scales[i, g] = scales[:, j * P : (j + 1) * P]
 
         o_banks, o_rows = {}, {}
         o_total = keep.tile([P, R], F32, name="o_total")
 
         def scores(i):
-            o_banks[i] = sum_bank()
-            for g in range(NG):
+            o_banks[i] = take_bank(("o", i))
+            for g in range(D_GROUPS):
                 nc.tensor.matmul_mx(
                     out=o_banks[i][:],
                     lhsT=d_codes[i, g].bitcast(E5M2),
-                    lhsT_scale=d_plane[i, g],
+                    lhsT_scale=d_scales[i, g],
                     rhs=model_codes[g][:].bitcast(E4M3),
-                    rhs_scale=model_plane[g][:],
+                    rhs_scale=model_scales[g][:],
                     start=(g == 0),
-                    stop=(g == NG - 1),
+                    stop=(g == D_GROUPS - 1),
                 )
 
         def o_copy(i):
-            o_rows[i] = keep.tile([P, R], F32, name="o_rows", tag="o%d" % i)
+            o_rows[i] = keep.tile([P, R], F32, name="o_rows", tag="o_rows%d" % i)
             nc.scalar.copy(out=o_rows[i][:], in_=o_banks[i][:])
+            give_bank(("o", i))
 
-        def o_add(i, source):
+        def o_add(i, engine, source):
+            so_far = o_rows[0] if i == 1 else o_total
+            engine.tensor_tensor(out=o_total[:], in0=so_far[:], in1=source[:], op=ALU.add)
+
+        def scores_aside(i):
+            scores(i)
+            o_copy(i)
             if i > 0:
-                so_far = o_rows[0] if i == 1 else o_total
-                nc.vector.tensor_tensor(out=o_total[:], in0=so_far[:], in1=source[:], op=ALU.add)
+                o_add(i, nc.gpsimd, o_rows[i])
 
-        PAIR, SINGLE = (0, 1), (2,)
-        LAST = TILES - 1
-
+        warm = take_bank("warm")
+        keep_warm(warm, WARM_UP[0])
+        for g in range(D_GROUPS):
+            spread_rel(g)
+        keep_warm(warm, WARM_UP[1])
+        x_sort(1, nc.vector.tensor_copy)
+        x_turn(0)
+        keep_warm(warm, WARM_UP[2])
+        give_bank("warm")
+        x_turn(1)
         for i in range(2):
-            x_turn(i)
-            x_copy(i, 0)
-            x_copy(i, 1)
-            x_quant(i)
-        for g in range(KG):
-            for nb in range(NG):
-                sim_pass(0, nb, g)
-        model_group(0)
-        for nb in range(NG):
-            row_sum(0, nb)
-        sim_bank(1, 0)
+            x_finish(i)
+            x_quantise(i)
+        x_sort(2, nc.vector.tensor_copy)
+        for b in range(2):
+            for i in range(2):
+                sim_bank(i, b)
+                row_sum(i, b)
         x_turn(2)
-        for g in range(NG):
-            d_make(0, g)
-        model_quant(0)
-
-        for i in range(1, TILES):
-            if i == 4:
-                scores(1)
-            if i >= 2:
-                d_copy(i - 2, PAIR)
-                d_copy(i - 2, SINGLE)
-                d_quant(i - 2, PAIR)
-                d_quant(i - 2, SINGLE)
-            if i == 4:
-                o_copy(1)
-                o_add(1, o_rows[1])
-            if i > 1:
-                sim_bank(i, 0)
-            row_sum(i, 0)
-            if i < LAST:
-                x_copy(i + 1, 0)
-            sim_bank(i, 1)
-            row_sum(i, 1)
-            if i < LAST:
-                x_copy(i + 1, 1)
-            if i == 2:
-                model_group(2)
-            if i < LAST:
-                x_quant(i + 1)
-            if i == 1:
-                model_group(1)
+        x_finish(2)
+        model_interleave(0)
+        x_quantise(2)
+        for i in range(2):
             sim_bank(i, 2)
             row_sum(i, 2)
-            if i == LAST:
-                break
-            for g in range(NG):
+            x_sort(i + SORT_LEAD, nc.scalar.copy)
+        sim_bank(2, 0)
+        d_make(0, 0)
+        x_turn(3)
+        d_make(0, 1)
+        d_make(0, 2)
+        d_turn(0, FRONT)
+        d_turn(0, BACK)
+        for g in range(D_GROUPS):
+            d_make(1, g)
+        model_quantise(0)
+
+        for i in range(2, LAST):
+            x_finish(i + 1)
+            x_quantise(i + 1)
+            if i <= D_GROUPS:
+                model_interleave(i - 1)
+            if i + 2 == LAST:
+                x_sort(LAST, nc.vector.tensor_copy)
+            if i > 2:
+                sim_bank(i, 0)
+            row_sum(i, 0)
+            d_finish(i - 2, FRONT)
+            sim_bank(i, 1)
+            row_sum(i, 1)
+            d_finish(i - 2, BACK)
+            d_quantise(i - 2, FRONT)
+            d_quantise(i - 2, BACK)
+            sim_bank(i, 2)
+            row_sum(i, 2)
+            for g in range(D_GROUPS):
                 d_make(i, g)
-            if i in (1, 2):
-                model_quant(i)
-            if i >= 3:
-                j = 0 if i == 3 else i - 2
-                scores(j)
-                o_copy(j)
-                o_add(j, o_rows[j])
-            d_turn(i - 1, PAIR)
-            d_turn(i - 1, SINGLE)
-            if i + 2 < TILES:
+            if i >= SCORE_LAG:
+                scores_aside(i - SCORE_LAG)
+            if i <= D_GROUPS:
+                model_quantise(i - 1)
+            if i + SORT_LEAD < LAST:
+                x_sort(i + SORT_LEAD, nc.scalar.copy)
+            d_turn(i - 1, FRONT)
+            d_turn(i - 1, BACK)
+            if i + 2 <= LAST:
                 x_turn(i + 2)
 
-        d_turn(LAST - 1, PAIR)
-        d_turn(LAST - 1, SINGLE)
-        d_copy(LAST - 1, PAIR)
-        d_copy(LAST - 1, SINGLE)
-        scores(LAST - 2)
+        scores(LAST - 4)
+        for groups in (FRONT, BACK):
+            d_finish(LAST - 2, groups)
+        for groups in (FRONT, BACK):
+            d_quantise(LAST - 2, groups)
+        o_copy(LAST - 4)
+        o_add(LAST - 4, nc.gpsimd, o_rows[LAST - 4])
+        for b in range(D_GROUPS):
+            sim_bank(LAST, b)
+            row_sum(LAST, b)
+        for step in (d_turn, d_finish):
+            step(LAST - 1, FRONT)
+            step(LAST - 1, BACK)
+        scores_aside(LAST - 3)
         d_make(LAST, 0)
-        d_quant(LAST - 1, PAIR)
-        d_quant(LAST - 1, SINGLE)
-        d_turn(LAST, (0,))
-        d_copy(LAST, (0,))
+        d_quantise(LAST - 1, FRONT)
+        d_quantise(LAST - 1, BACK)
+        scores(LAST - 2)
         o_copy(LAST - 2)
         d_make(LAST, 1)
-        scores(LAST - 1)
-        o_copy(LAST - 1)
-        d_turn(LAST, (1,))
-        d_copy(LAST, (1,))
         d_make(LAST, 2)
-        d_turn(LAST, (2,))
-        d_copy(LAST, (2,))
-        d_quant(LAST, (0,))
-        o_add(LAST - 2, o_rows[LAST - 2])
-        d_quant(LAST, (1,))
-        d_quant(LAST, (2,))
-        o_add(LAST - 1, o_rows[LAST - 1])
+        for g in range(D_GROUPS):
+            d_turn(LAST, (g,))
+            d_finish(LAST, (g,))
+        scores(LAST - 1)
+        d_quantise(LAST, (0,))
+        o_add(LAST - 2, nc.vector, o_rows[LAST - 2])
+        d_quantise(LAST, (1,))
+        d_quantise(LAST, (2,))
+        o_add(LAST - 1, nc.vector, o_banks[LAST - 1])
+        o_copy(LAST - 1)
         scores(LAST)
-        o_add(LAST, o_banks[LAST])
-        o_copy(LAST)
 
-        col_mean = turn_bank()
-        nc.tensor.matmul(col_mean[:], lhsT=mean_weights[:], rhs=o_total[:], start=True, stop=True)
+        col_mean = take_bank("mean")
+        halves = (slice(0, R // 2), slice(R // 2, R))
+        grand_total = keep.tile([P, R], F32, name="grand_total")
+        for half in halves:
+            nc.vector.tensor_tensor(
+                out=grand_total[:, half], in0=o_total[:, half], in1=o_banks[LAST][:, half], op=ALU.add
+            )
+        o_copy(LAST)
+        for half in halves:
+            nc.tensor.matmul(col_mean[:, half], lhsT=mean_weights[:], rhs=grand_total[:, half], start=True, stop=True)
         for i in range(TILES):
             result = work.tile([P, R], F32, name="result", bufs=TILES)
             nc.vector.tensor_tensor(out=result[:], in0=o_rows[i][:], in1=col_mean[:], op=ALU.subtract)

@@ -25,6 +25,7 @@ X_GROUPS = K // GROUP
 D_GROUPS = N // GROUP
 FRONT, BACK = (0, 1), (2,)
 SCORE_LAG = 4
+QUANTISE_LAG = 3
 SORT_LEAD = 3
 WARM_UP = (3, 1, 2)
 
@@ -240,7 +241,7 @@ def tile_centred_pattern_distances_s9_kernel(tc, x, w_words, w_scales, rel, mode
 
         def d_finish(i, groups):
             n = len(groups)
-            d_turned[i, groups] = work.tile([P, n * GROUP], BF16, name="d_turned", bufs=4, align_bytes=64)
+            d_turned[i, groups] = work.tile([P, n * GROUP], BF16, name="d_turned", bufs=6, align_bytes=64)
             nc.scalar.copy(
                 out=d_turned[i, groups][:].bitcast(F32).rearrange("p (g r u) -> p g r u", g=n, u=2),
                 in_=d_banks[i, groups][:, : n * 2 * P].rearrange("p (g u r) -> p g r u", g=n, u=2),
@@ -329,8 +330,8 @@ def tile_centred_pattern_distances_s9_kernel(tc, x, w_words, w_scales, rel, mode
             x_quantise(i + 1)
             if i <= D_GROUPS:
                 model_interleave(i - 1)
-            if i + 2 == LAST:
-                x_sort(LAST, nc.vector.tensor_copy)
+            if LAST - 1 <= i + 2 <= LAST:
+                x_sort(i + 2, nc.vector.tensor_copy)
             if i > 2:
                 sim_bank(i, 0)
             row_sum(i, 0)
@@ -338,17 +339,21 @@ def tile_centred_pattern_distances_s9_kernel(tc, x, w_words, w_scales, rel, mode
             sim_bank(i, 1)
             row_sum(i, 1)
             d_finish(i - 2, BACK)
-            d_quantise(i - 2, FRONT)
-            d_quantise(i - 2, BACK)
+            if i >= QUANTISE_LAG:
+                d_quantise(i - QUANTISE_LAG, FRONT)
+                d_quantise(i - QUANTISE_LAG, BACK)
             sim_bank(i, 2)
             row_sum(i, 2)
             for g in range(D_GROUPS):
                 d_make(i, g)
+            if i == LAST - 1:
+                d_quantise(i - 2, FRONT)
+                d_quantise(i - 2, BACK)
             if i >= SCORE_LAG:
                 scores_aside(i - SCORE_LAG)
             if i <= D_GROUPS:
                 model_quantise(i - 1)
-            if i + SORT_LEAD < LAST:
+            if i + SORT_LEAD < LAST - 1:
                 x_sort(i + SORT_LEAD, nc.scalar.copy)
             d_turn(i - 1, FRONT)
             d_turn(i - 1, BACK)
@@ -365,39 +370,39 @@ def tile_centred_pattern_distances_s9_kernel(tc, x, w_words, w_scales, rel, mode
         for b in range(D_GROUPS):
             sim_bank(LAST, b)
             row_sum(LAST, b)
+        scores_aside(LAST - 3)
         for step in (d_turn, d_finish):
             step(LAST - 1, FRONT)
             step(LAST - 1, BACK)
-        scores_aside(LAST - 3)
-        d_make(LAST, 0)
-        d_quantise(LAST - 1, FRONT)
-        d_quantise(LAST - 1, BACK)
+        for g in range(D_GROUPS):
+            d_make(LAST, g)
         scores(LAST - 2)
         o_copy(LAST - 2)
-        d_make(LAST, 1)
-        d_make(LAST, 2)
         for g in range(D_GROUPS):
             d_turn(LAST, (g,))
             d_finish(LAST, (g,))
+        d_quantise(LAST - 1, FRONT)
+        d_quantise(LAST - 1, BACK)
         scores(LAST - 1)
-        d_quantise(LAST, (0,))
         o_add(LAST - 2, nc.vector, o_rows[LAST - 2])
-        d_quantise(LAST, (1,))
-        d_quantise(LAST, (2,))
+        for g in range(D_GROUPS):
+            d_quantise(LAST, (g,))
         o_add(LAST - 1, nc.vector, o_banks[LAST - 1])
         o_copy(LAST - 1)
         scores(LAST)
 
         col_mean = take_bank("mean")
         halves = (slice(0, R // 2), slice(R // 2, R))
-        grand_total = keep.tile([P, R], F32, name="grand_total")
+        grand_total = []
         for half in halves:
+            part = work.tile([P, R // 2], F32, name="grand_total")
+            grand_total.append(part)
             nc.vector.tensor_tensor(
-                out=grand_total[:, half], in0=o_total[:, half], in1=o_banks[LAST][:, half], op=ALU.add
+                out=part[:], in0=o_total[:, half], in1=o_banks[LAST][:, half], op=ALU.add
             )
         o_copy(LAST)
-        for half in halves:
-            nc.tensor.matmul(col_mean[:, half], lhsT=mean_weights[:], rhs=grand_total[:, half], start=True, stop=True)
+        for half, part in zip(halves, grand_total):
+            nc.tensor.matmul(col_mean[:, half], lhsT=mean_weights[:], rhs=part[:], start=True, stop=True)
         for i in range(TILES):
             result = work.tile([P, R], F32, name="result", bufs=TILES)
             nc.vector.tensor_tensor(out=result[:], in0=o_rows[i][:], in1=col_mean[:], op=ALU.subtract)

@@ -26,6 +26,7 @@ D_GROUPS = N // GROUP
 FRONT, BACK = (0, 1), (2,)
 SCORE_LAG = 4
 QUANTISE_LAG = 3
+BLOCK_TURNED = 6
 SORT_LEAD = 3
 WARM_UP = (3, 1, 2)
 
@@ -75,6 +76,16 @@ def tile_centred_pattern_distances_s9_kernel(tc, x, w_words, w_scales, rel, mode
             x_rows[i] = keep.tile([P, K], BF16, name="x_rows", tag="x_rows%d" % i)
             nc.sync.dma_start(out=x_rows[i][:], in_=x[i * P : (i + 1) * P, :])
 
+        def load_x_blocks(i):
+            x_rows[i] = keep.tile([P, X_GROUPS, 4, P], BF16, name="x_rows", tag="x_rows%d" % i)
+            for g in range(X_GROUPS):
+                for a in range(4):
+                    first = GROUP * g + P * a
+                    nc.sync.dma_start(
+                        out=x_rows[i][32 * a : 32 * (a + 1), g, :, :],
+                        in_=x[i * P : (i + 1) * P, first : first + P].rearrange("(q j) k -> j q k", j=32),
+                    )
+
         def load_w_scales(plane, first):
             cols = slice(first, first + plane.shape[2])
             for q in range(4):
@@ -107,8 +118,8 @@ def tile_centred_pattern_distances_s9_kernel(tc, x, w_words, w_scales, rel, mode
         for g in range(D_GROUPS):
             load_model(g)
             load_x(3 + g)
-        for i in range(3 + D_GROUPS, TILES):
-            load_x(i)
+        for i in range(BLOCK_TURNED, TILES):
+            load_x_blocks(i)
 
         def w_scale(g, b):
             return w_planes[0][:, g, :] if b == 0 else w_planes[1][:, g, GROUP * (b - 1) : GROUP * b]
@@ -152,6 +163,28 @@ def tile_centred_pattern_distances_s9_kernel(tc, x, w_words, w_scales, rel, mode
                     else:
                         pairs = x_sorted[i][:, (2 * g + u) * P : (2 * g + u + 1) * P]
                     nc.tensor.transpose(x_banks[i, h][:, j * P : (j + 1) * P], pairs, ident[:])
+
+        x_blocks = {}
+
+        def x_sort_blocks(i):
+            x_sorted[i] = work.tile([P, K // 2], F32, name="x_sorted_blocks", align_bytes=64)
+            pairs = x_rows[i][:].rearrange("p g q k -> p (g q k)").bitcast(F32)
+            nc.vector.tensor_copy(
+                out=x_sorted[i][:].rearrange("p (m u c) -> p m u c", u=2, c=32),
+                in_=pairs.rearrange("p (m c u) -> p m u c", u=2, c=32),
+            )
+
+        def x_turn_blocks(i):
+            x_blocks[i] = work.tile([P, K // 2], F32, name="x_blocks", align_bytes=64)
+            nc.vector.transpose(out=x_blocks[i][:], in_=x_sorted[i][:])
+
+        def x_finish_blocks(i):
+            for h in range(2):
+                x_turned[i, h] = work.tile([P, K // 2], BF16, name="x_turned", bufs=4, align_bytes=64)
+                nc.scalar.copy(
+                    out=x_turned[i, h][:].bitcast(F32).rearrange("p (m j u) -> p m j u", j=32, u=2),
+                    in_=x_blocks[i][:, h * GROUP : (h + 1) * GROUP].rearrange("p (m u j) -> p m j u", j=32, u=2),
+                )
 
         def x_finish(i):
             for h in range(2):
@@ -319,29 +352,34 @@ def tile_centred_pattern_distances_s9_kernel(tc, x, w_words, w_scales, rel, mode
         x_turn(3)
         d_make(0, 1)
         d_make(0, 2)
+        sim_bank(2, 1)
+        d_make(1, 0)
         d_turn(0, FRONT)
         d_turn(0, BACK)
-        for g in range(D_GROUPS):
+        for g in range(1, D_GROUPS):
             d_make(1, g)
         model_quantise(0)
 
         for i in range(2, LAST):
-            x_finish(i + 1)
+            (x_finish if i + 1 < BLOCK_TURNED else x_finish_blocks)(i + 1)
             x_quantise(i + 1)
+            if BLOCK_TURNED <= i + 2 <= LAST:
+                x_sort_blocks(i + 2)
             if i <= D_GROUPS:
                 model_interleave(i - 1)
-            if LAST - 1 <= i + 2 <= LAST:
-                x_sort(i + 2, nc.vector.tensor_copy)
             if i > 2:
                 sim_bank(i, 0)
             row_sum(i, 0)
             d_finish(i - 2, FRONT)
-            sim_bank(i, 1)
+            if i > 2:
+                sim_bank(i, 1)
             row_sum(i, 1)
             d_finish(i - 2, BACK)
             if i >= QUANTISE_LAG:
                 d_quantise(i - QUANTISE_LAG, FRONT)
                 d_quantise(i - QUANTISE_LAG, BACK)
+            if BLOCK_TURNED <= i + 2 <= LAST:
+                x_turn_blocks(i + 2)
             sim_bank(i, 2)
             row_sum(i, 2)
             for g in range(D_GROUPS):
@@ -353,11 +391,11 @@ def tile_centred_pattern_distances_s9_kernel(tc, x, w_words, w_scales, rel, mode
                 scores_aside(i - SCORE_LAG)
             if i <= D_GROUPS:
                 model_quantise(i - 1)
-            if i + SORT_LEAD < LAST - 1:
+            if i + SORT_LEAD < BLOCK_TURNED:
                 x_sort(i + SORT_LEAD, nc.scalar.copy)
             d_turn(i - 1, FRONT)
             d_turn(i - 1, BACK)
-            if i + 2 <= LAST:
+            if i + 2 < BLOCK_TURNED:
                 x_turn(i + 2)
 
         scores(LAST - 4)

@@ -28,7 +28,6 @@ SCORE_LAG = 4
 QUANTISE_LAG = 3
 BLOCK_TURNED = 6
 SORT_LEAD = 3
-WARM_UP = (3, 1, 2)
 
 
 def tile_centred_pattern_distances_s9_kernel(tc, x, w_words, w_scales, rel, model, out):
@@ -49,8 +48,6 @@ def tile_centred_pattern_distances_s9_kernel(tc, x, w_words, w_scales, rel, mode
         def give_bank(owner):
             free_banks.append(bank_of.pop(owner))
 
-        zeros = keep.tile([P, GROUP], BF16, name="zeros")
-        nc.vector.memset(zeros[:], 0.0)
         ones = keep.tile([P, P], F32, name="ones")
         nc.vector.memset(ones[:], 1.0)
         w_planes = []
@@ -123,10 +120,6 @@ def tile_centred_pattern_distances_s9_kernel(tc, x, w_words, w_scales, rel, mode
 
         def w_scale(g, b):
             return w_planes[0][:, g, :] if b == 0 else w_planes[1][:, g, GROUP * (b - 1) : GROUP * b]
-
-        def keep_warm(bank, count):
-            for j in range(count):
-                nc.tensor.matmul(bank[:], lhsT=zeros[:, :P], rhs=zeros[:], start=True, stop=True)
 
         neg_rel = {}
 
@@ -321,15 +314,10 @@ def tile_centred_pattern_distances_s9_kernel(tc, x, w_words, w_scales, rel, mode
             if i > 0:
                 o_add(i, nc.gpsimd, o_rows[i])
 
-        warm = take_bank("warm")
-        keep_warm(warm, WARM_UP[0])
         for g in range(D_GROUPS):
             spread_rel(g)
-        keep_warm(warm, WARM_UP[1])
         x_sort(1, nc.vector.tensor_copy)
         x_turn(0)
-        keep_warm(warm, WARM_UP[2])
-        give_bank("warm")
         x_turn(1)
         for i in range(2):
             x_finish(i)

from contextlib import ExitStack

import concourse.mybir as mybir
from concourse.masks import make_identity

M, K, N, R = 1024, 2048, 1536, 512
FLOPS = 2 * M * K * N + 2 * M * N * R

F32 = mybir.dt.float32
BF16 = mybir.dt.bfloat16
I32 = mybir.dt.int32
U32 = mybir.dt.uint32
U8 = mybir.dt.uint8
E4M3 = mybir.dt.float8_e4m3fn_x4
E5M2 = mybir.dt.float8_e5m2_x4
E2M1 = mybir.dt.float4_e2m1fn_x4
ALU = mybir.AluOpType
IDENTITY = mybir.ActivationFunctionType.Identity

P = 128
GROUP = 512
TILES = M // P
LAST = TILES - 1
X_GROUPS = K // GROUP
D_GROUPS = N // GROUP
FRONT, BACK = (0, 1), (2,)
SCORE_LAG = 4
QUANTISE_LAG = 3
BLOCK_TURNED = 6
SORT_LEAD = 3


def tile_centred_pattern_distances_s9_kernel(tc, x, w_words, w_scales, rel, model, out):
    nc = tc.nc
    with ExitStack() as ctx:
        keep = ctx.enter_context(tc.tile_pool(name="keep", bufs=1))
        work = ctx.enter_context(tc.tile_pool(name="work", bufs=3))
        psum = ctx.enter_context(tc.psum_pool(name="psum", bufs=1))
        ctx.enter_context(tc.manual_schedule())

        free_banks, bank_of = list(range(8)), {}

        def take_bank(owner):
            bank_of[owner] = free_banks.pop(0)
            bank = psum.tile([P, GROUP], F32, name="bank", tag="bank%d" % bank_of[owner])
            return bank

        def give_bank(owner):
            free_banks.append(bank_of.pop(owner))

        ones = keep.tile([P, P], F32, name="ones")
        nc.vector.memset(ones[:], 1.0)
        w_planes = []
        for banks in (1, D_GROUPS - 1):
            plane = keep.tile([P, X_GROUPS, banks * GROUP], U8, name="w_plane", tag="w_plane%d" % banks, align_bytes=64)
            nc.vector.memset(plane[:].bitcast(I32), 0)
            w_planes.append(plane)
        ident = keep.tile([P, P], F32, name="ident")
        make_identity(nc, ident[:])
        ident_bf = keep.tile([P, P], BF16, name="ident_bf")
        make_identity(nc, ident_bf[:])
        rel_cols = keep.tile([P, D_GROUPS * 4], BF16, name="rel_cols")
        nc.scalar.dma_start(
            out=rel_cols[:].rearrange("p (g t) -> p g t", t=4),
            in_=rel.rearrange("(g p t) -> p g t", p=P, t=4),
        )
        mean_weights = keep.tile([P, P], F32, name="mean_weights")
        nc.scalar.activation(out=mean_weights[:], in_=ones[:], func=IDENTITY, scale=1.0 / M)

        x_rows, w_codes, model_rows = {}, {}, {}

        def load_x(i):
            x_rows[i] = keep.tile([P, K], BF16, name="x_rows", tag="x_rows%d" % i)
            nc.sync.dma_start(out=x_rows[i][:], in_=x[i * P : (i + 1) * P, :])

        def load_x_blocks(i):
            x_rows[i] = keep.tile([P, X_GROUPS, 4, P], BF16, name="x_rows", tag="x_rows%d" % i)
            for g in range(X_GROUPS):
                for a in range(4):
                    first = GROUP * g + P * a
                    nc.sync.dma_start(
                        out=x_rows[i][32 * a : 32 * (a + 1), g, :, :],
                        in_=x[i * P : (i + 1) * P, first : first + P].rearrange("(q j) k -> j q k", j=32),
                    )

        def load_w_scales(plane, first):
            cols = slice(first, first + plane.shape[2])
            for q in range(4):
                nc.sync.dma_start(
                    out=plane[32 * q : 32 * q + 4, :, :].bitcast(I32),
                    in_=w_scales[:, 4 * q : 4 * q + 4, cols].bitcast(I32).rearrange("g r n -> r g n"),
                )

        def load_w_codes(b):
            w_codes[b] = keep.tile([P, X_GROUPS, 2 * GROUP], U8, name="w_codes", tag="w_codes%d" % b, align_bytes=64)
            nc.sync.dma_start(
                out=w_codes[b][:].bitcast(I32),
                in_=w_words[:, :, 2 * GROUP * b : 2 * GROUP * (b + 1)].bitcast(I32).rearrange("g p n -> p g n"),
            )

        def load_model(g):
            model_rows[g] = keep.tile([P, 4, R], BF16, name="model_rows", tag="model_rows%d" % g)
            nc.sync.dma_start(
                out=model_rows[g][:], in_=model[GROUP * g : GROUP * (g + 1), :].rearrange("(p t) r -> p t r", t=4)
            )

        load_x(0)
        load_x(1)
        load_w_scales(w_planes[0], 0)
        load_w_codes(0)
        load_w_scales(w_planes[1], GROUP)
        load_w_codes(1)
        load_x(2)
        load_w_codes(2)
        for g in range(D_GROUPS):
            load_model(g)
            load_x(3 + g)
        for i in range(BLOCK_TURNED, TILES):
            load_x_blocks(i)

        def w_scale(g, b):
            return w_planes[0][:, g, :] if b == 0 else w_planes[1][:, g, GROUP * (b - 1) : GROUP * b]

        neg_rel = {}

        def spread_rel(g):
            bank = take_bank("rel")
            for t in range(4):
                column = rel_cols[:, 4 * g + t : 4 * g + t + 1].to_broadcast([P, P])
                nc.tensor.matmul(bank[:, t * P : (t + 1) * P], lhsT=column, rhs=ident_bf[:], start=True, stop=True)
            neg_rel[g] = keep.tile([P, GROUP], BF16, name="neg_rel", tag="neg_rel%d" % g)
            nc.scalar.activation(
                out=neg_rel[g][:].rearrange("p (u c e) -> p u c e", u=2, e=2),
                in_=bank[:].rearrange("p (u e c) -> p u c e", u=2, e=2),
                func=IDENTITY,
                scale=-1.0,
            )
            give_bank("rel")

        x_sorted, x_banks, x_turned, x_codes, x_scales = {}, {}, {}, {}, {}

        def x_sort(i, copy):
            x_sorted[i] = work.tile([P, K // 2], F32, name="x_sorted")
            copy(
                out=x_sorted[i][:].rearrange("p (g u c) -> p g u c", g=X_GROUPS, u=2),
                in_=x_rows[i][:].bitcast(F32).rearrange("p (g c u) -> p g u c", g=X_GROUPS, u=2),
            )

        def x_turn(i):
            for h in range(2):
                x_banks[i, h] = take_bank(("x", i, h))
                for j in range(4):
                    g, u = 2 * h + j // 2, j % 2
                    if i == 0:
                        pairs = x_rows[i][:].bitcast(F32)[:, 2 * P * g + u : 2 * P * (g + 1) : 2]
                    else:
                        pairs = x_sorted[i][:, (2 * g + u) * P : (2 * g + u + 1) * P]
                    nc.tensor.transpose(x_banks[i, h][:, j * P : (j + 1) * P], pairs, ident[:])

        x_blocks = {}

        def x_sort_blocks(i):
            x_sorted[i] = work.tile([P, K // 2], F32, name="x_sorted_blocks", align_bytes=64)
            pairs = x_rows[i][:].rearrange("p g q k -> p (g q k)").bitcast(F32)
            nc.vector.tensor_copy(
                out=x_sorted[i][:].rearrange("p (m u c) -> p m u c", u=2, c=32),
                in_=pairs.rearrange("p (m c u) -> p m u c", u=2, c=32),
            )

        def x_turn_blocks(i):
            x_blocks[i] = work.tile([P, K // 2], F32, name="x_blocks", align_bytes=64)
            nc.vector.transpose(out=x_blocks[i][:], in_=x_sorted[i][:])

        def x_finish_blocks(i):
            for h in range(2):
                x_turned[i, h] = work.tile([P, K // 2], BF16, name="x_turned", bufs=4, align_bytes=64)
                nc.scalar.copy(
                    out=x_turned[i, h][:].bitcast(F32).rearrange("p (m j u) -> p m j u", j=32, u=2),
                    in_=x_blocks[i][:, h * GROUP : (h + 1) * GROUP].rearrange("p (m u j) -> p m j u", j=32, u=2),
                )

        def x_finish(i):
            for h in range(2):
                x_turned[i, h] = work.tile([P, K // 2], BF16, name="x_turned", bufs=4, align_bytes=64)
                nc.scalar.copy(
                    out=x_turned[i, h][:].bitcast(F32).rearrange("p (g r u) -> p g r u", g=2, u=2),
                    in_=x_banks[i, h][:].rearrange("p (g u r) -> p g r u", g=2, u=2),
                )
                give_bank(("x", i, h))

        def x_quantise(i):
            for h in range(2):
                x_codes[i, h] = work.tile([P, 2 * P], U32, name="x_codes", bufs=6, align_bytes=64)
                x_scales[i, h] = work.tile([P, 2 * P], U8, name="x_scales", bufs=6, align_bytes=64)
                nc.vector.quantize_mx(
                    out=x_codes[i, h][:].bitcast(E4M3), scales=x_scales[i, h][:], in_=x_turned[i, h][:]
                )

        model_words, model_codes, model_scales = {}, {}, {}

        def model_interleave(g):
            model_words[g] = keep.tile([P, 4 * R], BF16, name="model_words", tag="model_words%d" % g, align_bytes=64)
            nc.vector.tensor_copy(
                out=model_words[g][:].rearrange("p (c i t) -> p c t i", i=4, t=4),
                in_=model_rows[g][:].rearrange("p t (c i) -> p c t i", i=4),
            )

        def model_quantise(g):
            model_codes[g] = keep.tile([P, R], U32, name="model_codes", tag="model_codes%d" % g, align_bytes=64)
            model_scales[g] = keep.tile([P, R], U8, name="model_scales", tag="model_scales%d" % g, align_bytes=64)
            nc.vector.quantize_mx(
                out=model_codes[g][:].bitcast(E4M3), scales=model_scales[g][:], in_=model_words[g][:]
            )

        sim, row_mean, d_rows = {}, {}, {}

        def sim_bank(i, b):
            sim[i, b] = take_bank(("sim", i, b))
            for g in range(X_GROUPS):
                probes = slice(g % 2 * P, (g % 2 + 1) * P)
                nc.tensor.matmul_mx(
                    out=sim[i, b][:],
                    lhsT=x_codes[i, g // 2][:, probes].bitcast(E4M3),
                    lhsT_scale=x_scales[i, g // 2][:, probes],
                    rhs=w_codes[b][:, g, :].bitcast(E2M1),
                    rhs_scale=w_scale(g, b),
                    start=(g == 0),
                    stop=(g == X_GROUPS - 1),
                )

        def row_sum(i, b):
            unread = work.tile([P, GROUP], BF16, name="unread")
            total = work.tile([P, 1], F32, name="total", bufs=8)
            nc.scalar.activation(
                out=unread[:],
                in_=sim[i, b][:],
                func=IDENTITY,
                scale=1.0 / (N * GROUP ** (D_GROUPS - 1 - b)),
                bias=row_mean[i][:] if b else 0.0,
                accum_out=total[:],
            )
            row_mean[i] = total

        def d_make(i, g):
            d_rows[i, g] = work.tile([P, GROUP], BF16, name="d_rows", bufs=9)
            for u in range(2):
                half = slice(2 * P * u, 2 * P * (u + 1))
                nc.vector.scalar_tensor_tensor(
                    out=d_rows[i, g][:, half].rearrange("p (c e) -> p c e", e=2),
                    in0=sim[i, g][:].rearrange("p (c u e) -> p u c e", u=2, e=2)[:, u],
                    scalar=row_mean[i][:],
                    in1=neg_rel[g][:, half].rearrange("p (c e) -> p c e", e=2),
                    op0=ALU.subtract,
                    op1=ALU.mult,
                )
            give_bank(("sim", i, g))

        d_banks, d_turned, d_codes, d_scales = {}, {}, {}, {}

        def d_turn(i, groups):
            d_banks[i, groups] = take_bank(("d", i, groups))
            for j, g in enumerate(groups):
                pairs = d_rows[i, g][:].bitcast(F32)
                for u in range(2):
                    col = (2 * j + u) * P
                    nc.tensor.transpose(d_banks[i, groups][:, col : col + P], pairs[:, u * P : (u + 1) * P], ident[:])

        def d_finish(i, groups):
            n = len(groups)
            d_turned[i, groups] = work.tile([P, n * GROUP], BF16, name="d_turned", bufs=6, align_bytes=64)
            nc.scalar.copy(
                out=d_turned[i, groups][:].bitcast(F32).rearrange("p (g r u) -> p g r u", g=n, u=2),
                in_=d_banks[i, groups][:, : n * 2 * P].rearrange("p (g u r) -> p g r u", g=n, u=2),
            )
            give_bank(("d", i, groups))

        def d_quantise(i, groups):
            n = len(groups)
            codes = work.tile([P, n * P], U32, name="d_codes", bufs=10, align_bytes=64)
            scales = work.tile([P, n * P], U8, name="d_scales", bufs=10, align_bytes=64)
            nc.vector.quantize_mx(out=codes[:].bitcast(E5M2), scales=scales[:], in_=d_turned[i, groups][:])
            for j, g in enumerate(groups):
                d_codes[i, g] = codes[:, j * P : (j + 1) * P]
                d_scales[i, g] = scales[:, j * P : (j + 1) * P]

        o_banks, o_rows = {}, {}
        o_total = keep.tile([P, R], F32, name="o_total")

        def scores(i):
            o_banks[i] = take_bank(("o", i))
            for g in range(D_GROUPS):
                nc.tensor.matmul_mx(
                    out=o_banks[i][:],
                    lhsT=d_codes[i, g].bitcast(E5M2),
                    lhsT_scale=d_scales[i, g],
                    rhs=model_codes[g][:].bitcast(E4M3),
                    rhs_scale=model_scales[g][:],
                    start=(g == 0),
                    stop=(g == D_GROUPS - 1),
                )

        def o_copy(i):
            o_rows[i] = keep.tile([P, R], F32, name="o_rows", tag="o_rows%d" % i)
            nc.scalar.copy(out=o_rows[i][:], in_=o_banks[i][:])
            give_bank(("o", i))

        def o_add(i, engine, source):
            so_far = o_rows[0] if i == 1 else o_total
            engine.tensor_tensor(out=o_total[:], in0=so_far[:], in1=source[:], op=ALU.add)

        def scores_aside(i):
            scores(i)
            o_copy(i)
            if i > 0:
                o_add(i, nc.gpsimd, o_rows[i])

        for g in range(D_GROUPS):
            spread_rel(g)
        x_sort(1, nc.vector.tensor_copy)
        x_turn(0)
        x_turn(1)
        for i in range(2):
            x_finish(i)
            x_quantise(i)
        x_sort(2, nc.vector.tensor_copy)
        for b in range(2):
            for i in range(2):
                sim_bank(i, b)
                row_sum(i, b)
        x_turn(2)
        x_finish(2)
        model_interleave(0)
        x_quantise(2)
        for i in range(2):
            sim_bank(i, 2)
            row_sum(i, 2)
            x_sort(i + SORT_LEAD, nc.scalar.copy)
        sim_bank(2, 0)
        d_make(0, 0)
        x_turn(3)
        d_make(0, 1)
        d_make(0, 2)
        sim_bank(2, 1)
        d_make(1, 0)
        d_turn(0, FRONT)
        d_turn(0, BACK)
        for g in range(1, D_GROUPS):
            d_make(1, g)
        model_quantise(0)

        for i in range(2, LAST):
            (x_finish if i + 1 < BLOCK_TURNED else x_finish_blocks)(i + 1)
            x_quantise(i + 1)
            if BLOCK_TURNED <= i + 2 <= LAST:
                x_sort_blocks(i + 2)
            if i <= D_GROUPS:
                model_interleave(i - 1)
            if i > 2:
                sim_bank(i, 0)
            row_sum(i, 0)
            d_finish(i - 2, FRONT)
            if i > 2:
                sim_bank(i, 1)
            row_sum(i, 1)
            d_finish(i - 2, BACK)
            if i >= QUANTISE_LAG:
                d_quantise(i - QUANTISE_LAG, FRONT)
                d_quantise(i - QUANTISE_LAG, BACK)
            if BLOCK_TURNED <= i + 2 <= LAST:
                x_turn_blocks(i + 2)
            sim_bank(i, 2)
            row_sum(i, 2)
            for g in range(D_GROUPS):
                d_make(i, g)
            if i == LAST - 1:
                d_quantise(i - 2, FRONT)
                d_quantise(i - 2, BACK)
            if i >= SCORE_LAG:
                scores_aside(i - SCORE_LAG)
            if i <= D_GROUPS:
                model_quantise(i - 1)
            if i + SORT_LEAD < BLOCK_TURNED:
                x_sort(i + SORT_LEAD, nc.scalar.copy)
            d_turn(i - 1, FRONT)
            d_turn(i - 1, BACK)
            if i + 2 < BLOCK_TURNED:
                x_turn(i + 2)

        scores(LAST - 4)
        for groups in (FRONT, BACK):
            d_finish(LAST - 2, groups)
        for groups in (FRONT, BACK):
            d_quantise(LAST - 2, groups)
        o_copy(LAST - 4)
        o_add(LAST - 4, nc.gpsimd, o_rows[LAST - 4])
        for b in range(D_GROUPS):
            sim_bank(LAST, b)
            row_sum(LAST, b)
        scores_aside(LAST - 3)
        for step in (d_turn, d_finish):
            step(LAST - 1, FRONT)
            step(LAST - 1, BACK)
        for g in range(D_GROUPS):
            d_make(LAST, g)
        scores(LAST - 2)
        o_copy(LAST - 2)
        for g in range(D_GROUPS):
            d_turn(LAST, (g,))
            d_finish(LAST, (g,))
        d_quantise(LAST - 1, FRONT)
        d_quantise(LAST - 1, BACK)
        scores(LAST - 1)
        o_add(LAST - 2, nc.vector, o_rows[LAST - 2])
        for g in range(D_GROUPS):
            d_quantise(LAST, (g,))
        o_add(LAST - 1, nc.vector, o_banks[LAST - 1])
        o_copy(LAST - 1)
        scores(LAST)

        col_mean = take_bank("mean")
        halves = (slice(0, R // 2), slice(R // 2, R))
        grand_total = []
        for half in halves:
            part = work.tile([P, R // 2], F32, name="grand_total")
            grand_total.append(part)
            nc.vector.tensor_tensor(
                out=part[:], in0=o_total[:, half], in1=o_banks[LAST][:, half], op=ALU.add
            )
        o_copy(LAST)
        for half, part in zip(halves, grand_total):
            nc.tensor.matmul(col_mean[:, half], lhsT=mean_weights[:], rhs=part[:], start=True, stop=True)
        for i in range(TILES):
            result = work.tile([P, R], F32, name="result", bufs=TILES)
            nc.vector.tensor_tensor(out=result[:], in0=o_rows[i][:], in1=col_mean[:], op=ALU.subtract)
            nc.sync.dma_start(out=out[i * P : (i + 1) * P, :], in_=result[:])
